import numpy as np, ml_dtypes
CORES = [89,94,345,350]
N = 4
import mx_ref
NC, WT = 128, 2
BF = ml_dtypes.bfloat16
def pk(c, s, i=0):
    return (np.ascontiguousarray(c[:, 512 * i:512 * i + 512]), mx_ref.live(s[:, 128 * i:128 * i + 128]))
def inputs(rng, e, E):
    def f(*shape):
        v = (rng.standard_normal(shape, dtype=np.float32) * np.exp2(rng.integers(-2, 3, shape[:-1] + (1,)))).astype(BF)
        return mx_ref.spread((v.astype(np.float32) * np.exp2(rng.integers(-E, E + 1, shape[:-2] + (1, 1))).astype(np.float32)).astype(BF), rng, e)
    def packed(k):
        c = np.zeros((N, 128, k * 512), np.uint8); s = np.zeros((N, 128, k * 128), np.uint8)
        for r in range(N):
            for i in range(k):
                a, b = mx_ref.quantize(f(128, 512)); c[r][:, 512 * i:512 * i + 512] = a; s[r][:, 128 * i:128 * i + 128] = mx_ref.plane(b, rng)
        return c, s
    d = {}
    d["wc"], d["ws"] = packed(WT)
    d["x"] = f(N, 128, 4 * NC)
    return d
def setup_inputs(rng):
    return inputs(rng, 0, 0)
def setup_inputs_blocks(rng):
    return inputs(rng, 4, 0)
def setup_inputs_wide(rng):
    return inputs(rng, 0, 8)
def reference(wc, ws, x):
    y = np.zeros((N, 128, N * WT * NC), np.float32)
    for r in range(N):
        X = mx_ref.quantize(x[r])
        for b in range(N * WT):
            y[r][:, NC * b:NC * b + NC] = mx_ref.matmul(pk(wc[b // WT], ws[b // WT], b % WT), X)
    return {"y": y}

@@ -1,0 +1,206 @@
+from concourse.bass import DstId, RemoteDMATransfer
+from concourse.mybir import dt
+
+NHOSTS = 4
+TW = 128
+
+SCRATCH = {
+    "xb": ("sbuf", [128, 512], "bfloat16"),
+    "xq": ("sbuf", [128, TW], "float8_e4m3fn_x4"),
+    "xs": ("sbuf", [128, TW], "uint8"),
+    "wq": ("sbuf", [128, 3 * TW], "float8_e4m3fn_x4"),
+    "wp": ("sbuf", [128, 3 * TW], "uint8"),
+    "st": ("sbuf", [128, 2 * TW], "float32"),
+    "ps": ("psum", [128, 8 * 512], "float32"),
+    "oc0": ("dram", [128, TW], "float8_e4m3fn_x4"), "oc1": ("dram", [128, TW], "float8_e4m3fn_x4"),
+    "op0": ("dram", [128, TW], "uint8"), "op1": ("dram", [128, TW], "uint8"),
+    "rc": ("dram", [128, TW], "float8_e4m3fn_x4"), "rp": ("dram", [128, TW], "uint8"),
+    "fc0": ("dram", [128, TW], "float8_e4m3fn_x4"), "fc1": ("dram", [128, TW], "float8_e4m3fn_x4"),
+    "fp0": ("dram", [128, TW], "uint8"), "fp1": ("dram", [128, TW], "uint8"),
+    "nc1": ("dram", [128, TW], "float8_e4m3fn_x4"), "np1": ("dram", [128, TW], "uint8"),
+}
+SEMAPHORES = (["ldp", "ldc", "ldx", "ldw", "qz", "snt", "rlp", "rlc", "cr", "n0", "n1", "r00", "r01", "r10", "r11",
+               "f3", "f6", "f7"]
+              + ["mm%d" % k for k in range(8)] + ["cp%d" % k for k in range(8)] + ["st%d" % k for k in range(8)])
+
+
+def _bits(mask):
+    return [1 << k for k in range(mask.bit_length()) if (mask >> k) & 1]
+
+
+def _join(bits):
+    m = 0
+    for b in bits:
+        m |= b
+    return m
+
+
+def _c8(ap):
+    return ap.bitcast(dt.uint8)
+
+
+def _plan(T, topo):
+    cores = list(T.cores)
+    per = topo.CORES_PER_HOST
+    info, relay = {}, {}
+    for s in cores:
+        here = [c for c in cores if topo.host(c) == topo.host(s)]
+        far = [c for c in cores if topo.host(c) != topo.host(s)]
+        twin = [c for c in far if topo.die(c) == topo.die(s)][0]
+        other = [c for c in far if c != twin][0]
+        mids = []
+        for m in range(NHOSTS):
+            image = s % per + m * per
+            if m in (topo.host(s), topo.host(twin)):
+                continue
+            if topo.may_write(s, image) and topo.may_write(image, twin):
+                mids.append(m)
+        rel = []
+        for m in mids[:2]:
+            images = [c % per + m * per for c in cores]
+            if topo.rack(m) == topo.rack(topo.host(s)):
+                k = s % per + m * per
+            else:
+                k = [c for c in range(m * per, (m + 1) * per)
+                     if topo.chip(c) == topo.chip(s) and topo.die(c) == topo.die(s) and c not in images][0]
+            rel.append(k)
+        info[s] = {"peer": [c for c in here if c != s][0], "twin": twin, "other": other, "pos": here.index(s), "relay": rel}
+        for i, k in enumerate(rel):
+            relay[k] = (s, i)
+    return info, relay
+
+
+def _dst(topo, d, src):
+    rid, pid = topo.addr(d, src)
+    return DstId(rid=rid, pnc=pid)
+
+
+def _relay(g, core, T, topo, info, s, i):
+    S = T.sem
+    twin, other = info[s]["twin"], info[s]["other"]
+    bits = _bits(topo.mask(core, twin) & topo.mask(core, other))
+    mask = _join(bits)
+    sem = S["r%d%d" % (info[s]["pos"], i)]
+    ids = [_dst(topo, twin, core), _dst(topo, other, core)]
+    g.wait_ge(S.rlp, 4)
+    g.wait_ge(S.cr, 1)
+    g.remote_dma_fused([RemoteDMATransfer(dst_ids=ids, dma_engine_mask=mask, remote_sem=sem, srcs=[T.rp[:]],
+                                          dsts=[T.wp[:, TW * i:TW * i + TW], T["fp%d" % i][:]])], local_sem=S.snt)
+    g.wait_ge(S.rlc, 4)
+    g.remote_dma_fused([RemoteDMATransfer(dst_ids=ids, dma_engine_mask=mask, remote_sem=sem, srcs=[_c8(T.rc[:])],
+                                          dsts=[_c8(T.wq[:, TW * i:TW * i + TW]), _c8(T["fc%d" % i][:])])], local_sem=S.snt)
+    g.wait_ge(S.snt, 2 * len(bits))
+
+
+def _rank(g, core, T, topo, info):
+    S = T.sem
+    me = info[core]
+    cores = list(T.cores)
+    r = T.rank_of(core)
+    peer, twin, other = me["peer"], me["twin"], me["other"]
+    rx, ry = me["relay"]
+
+    g.scalar.dma_start(T.op0[:], T.ws[:, 0:TW]).then_inc(S.ldp, 16)
+    g.scalar.dma_start(T.op1[:], T.ws[:, TW:2 * TW]).then_inc(S.ldp, 16)
+    g.sync.dma_start(_c8(T.oc0[:]), T.wc[:, 0:4 * TW]).then_inc(S.ldc, 16)
+    g.sync.dma_start(_c8(T.oc1[:]), T.wc[:, 4 * TW:8 * TW]).then_inc(S.ldc, 16)
+    g.scalar.dma_start(T.xb[:], T.x[:]).then_inc(S.ldx, 16)
+    g.sync.dma_start(_c8(T.wq[:, 0:2 * TW]), T.wc[:]).then_inc(S.ldw, 16)
+    g.scalar.dma_start(T.wp[:, 0:2 * TW], T.ws[:]).then_inc(S.ldw, 16)
+
+    off = _bits(topo.mask(core, rx) & topo.mask(core, ry))
+    ex, ey = off[0::2], off[1::2]
+    near = [b for b in _bits(topo.mask(core, peer)) if b not in off]
+    e0, e1 = near[0::2], near[1::2]
+    sent = 0
+    dx, dy, dp = _dst(topo, rx, core), _dst(topo, ry, core), _dst(topo, peer, core)
+    g.wait_ge(S.ldp, 32)
+    g.remote_dma_fused([
+        RemoteDMATransfer(dst_ids=[dx], dma_engine_mask=_join(ex), remote_sem=S.rlp, src=T.op0[:], dst=T.rp[:]),
+        RemoteDMATransfer(dst_ids=[dy], dma_engine_mask=_join(ey), remote_sem=S.rlp, src=T.op1[:], dst=T.rp[:]),
+    ], local_sem=S.snt)
+    g.wait_ge(S.ldc, 32)
+    g.remote_dma_fused([
+        RemoteDMATransfer(dst_ids=[dx], dma_engine_mask=_join(ex), remote_sem=S.rlc, src=_c8(T.oc0[:]), dst=_c8(T.rc[:])),
+        RemoteDMATransfer(dst_ids=[dy], dma_engine_mask=_join(ey), remote_sem=S.rlc, src=_c8(T.oc1[:]), dst=_c8(T.rc[:])),
+    ], local_sem=S.snt)
+    sent += 2 * (len(ex) + len(ey))
+    g.wait_ge(S.mm0, 1)
+    g.wait_ge(S.mm1, 1)
+    tx, ty = info[twin]["relay"]
+    g.remote_dma_fused([
+        RemoteDMATransfer(dst_ids=[_dst(topo, tx, core)], dma_engine_mask=ex[0], remote_sem=S.cr),
+        RemoteDMATransfer(dst_ids=[_dst(topo, ty, core)], dma_engine_mask=ey[0], remote_sem=S.cr),
+    ], local_sem=S.snt)
+    sent += 2
+    g.remote_dma_fused([
+        RemoteDMATransfer(dst_ids=[dp], dma_engine_mask=_join(e0), remote_sem=S.n0, src=T.op0[:], dst=T.wp[:, 2 * TW:3 * TW]),
+        RemoteDMATransfer(dst_ids=[dp], dma_engine_mask=_join(e1), remote_sem=S.n1, src=T.op1[:], dst=T.np1[:]),
+    ], local_sem=S.snt)
+    g.remote_dma_fused([
+        RemoteDMATransfer(dst_ids=[dp], dma_engine_mask=_join(e0), remote_sem=S.n0, src=_c8(T.oc0[:]),
+                          dst=_c8(T.wq[:, 2 * TW:3 * TW])),
+        RemoteDMATransfer(dst_ids=[dp], dma_engine_mask=_join(e1), remote_sem=S.n1, src=_c8(T.oc1[:]), dst=_c8(T.nc1[:])),
+    ], local_sem=S.snt)
+    sent += 2 * (len(e0) + len(e1))
+    g.wait_ge(S.snt, sent)
+
+    nrel = 2 * len(_bits(topo.mask(info[twin]["relay"][0], core)))
+    st_, so_ = "r%d" % info[twin]["pos"], "r%d" % info[other]["pos"]
+    rp_, rt_, ro_ = cores.index(peer), cores.index(twin), cores.index(other)
+    blocks = [
+        (0, r, 0, [(S.qz, 1), (S.ldw, 32)]),
+        (1, r, 1, []),
+        (2, rp_, 0, [(S.n0, 2 * len(e0))]),
+        (2, rp_, 1, [(S.f3, 32)]),
+        (0, rt_, 0, [(S[st_ + "0"], nrel)]),
+        (1, rt_, 1, [(S[st_ + "1"], nrel)]),
+        (2, ro_, 0, [(S.f6, 32)]),
+        (0, ro_, 1, [(S.f7, 32)]),
+    ]
+    g.vector.wait_ge(S.ldx, 16)
+    g.vector.quantize_mx(T.xq[:], T.xs[:], T.xb[:]).then_inc(S.qz, 1)
+    for k, (slot, j, i, waits) in enumerate(blocks):
+        b = 2 * j + i
+        for sem, val in waits:
+            g.tensor.wait_ge(sem, val)
+        g.tensor.matmul_mx(T.ps[:, 512 * b:512 * b + TW], T.wq[:, TW * slot:TW * slot + TW], T.wp[:, TW * slot:TW * slot + TW],
+                           T.xq[:], T.xs[:], True, True).then_inc(S["mm%d" % k], 1)
+        g.vector.wait_ge(S["mm%d" % k], 1)
+        if k >= 2:
+            g.vector.wait_ge(S["st%d" % (k - 2)], 16)
+        h = k % 2
+        g.vector.tensor_copy(T.st[:, TW * h:TW * h + TW], T.ps[:, 512 * b:512 * b + TW]).then_inc(S["cp%d" % k], 1)
+
+    def store(q, k):
+        b = 2 * blocks[k][1] + blocks[k][2]
+        h = k % 2
+        q.wait_ge(S["cp%d" % k], 1)
+        q.dma_start(T.y[:, TW * b:TW * b + TW], T.st[:, TW * h:TW * h + TW]).then_inc(S["st%d" % k], 16)
+
+    def fetch(q, codes, src, slot, free, arrived, count, done):
+        q.wait_ge(free, 1)
+        q.wait_ge(arrived, count)
+        if codes:
+            q.dma_start(_c8(T.wq[:, TW * slot:TW * slot + TW]), _c8(src[:])).then_inc(done, 16)
+        else:
+            q.dma_start(T.wp[:, TW * slot:TW * slot + TW], src[:]).then_inc(done, 16)
+
+    for q, codes, odd in ((g.sync, True, 0), (g.scalar, False, 1)):
+        store(q, 0 + odd)
+        fetch(q, codes, T.nc1 if codes else T.np1, 2, S.mm2, S.n1, 2 * len(e1), S.f3)
+        store(q, 2 + odd)
+        fetch(q, codes, T.fc0 if codes else T.fp0, 2, S.mm3, S[so_ + "0"], nrel, S.f6)
+        fetch(q, codes, T.fc1 if codes else T.fp1, 0, S.mm4, S[so_ + "1"], nrel, S.f7)
+        store(q, 4 + odd)
+        store(q, 6 + odd)
+        q.wait_ge(S["st%d" % (6 + odd)], 16)
+
+
+def rank_program(g, core, T, topo):
+    info, relay = _plan(T, topo)
+    if core in relay:
+        s, i = relay[core]
+        _relay(g, core, T, topo, info, s, i)
+    elif T.rank_of(core) is not None:
+        _rank(g, core, T, topo, info)

@@ -112,19 +112,14 @@ def _rank(g, core, T, topo, info):
     ex, ey = off[0::2], off[1::2]
     near = [b for b in _bits(topo.mask(core, peer)) if b not in off]
     e0, e1 = near[0::2], near[1::2]
-    sent = 0
     dx, dy, dp = _dst(topo, rx, core), _dst(topo, ry, core), _dst(topo, peer, core)
     g.wait_ge(S.ldp, 32)
     g.remote_dma_fused([
         RemoteDMATransfer(dst_ids=[dx], dma_engine_mask=_join(ex), remote_sem=S.rlp, src=T.op0[:], dst=T.rp[:]),
         RemoteDMATransfer(dst_ids=[dy], dma_engine_mask=_join(ey), remote_sem=S.rlp, src=T.op1[:], dst=T.rp[:]),
+        RemoteDMATransfer(dst_ids=[dp], dma_engine_mask=_join(e0), remote_sem=S.n0, src=T.op0[:], dst=T.wp[:, 2 * TW:3 * TW]),
+        RemoteDMATransfer(dst_ids=[dp], dma_engine_mask=_join(e1), remote_sem=S.n1, src=T.op1[:], dst=T.np1[:]),
     ], local_sem=S.snt)
-    g.wait_ge(S.ldc, 32)
-    g.remote_dma_fused([
-        RemoteDMATransfer(dst_ids=[dx], dma_engine_mask=_join(ex), remote_sem=S.rlc, src=_c8(T.oc0[:]), dst=_c8(T.rc[:])),
-        RemoteDMATransfer(dst_ids=[dy], dma_engine_mask=_join(ey), remote_sem=S.rlc, src=_c8(T.oc1[:]), dst=_c8(T.rc[:])),
-    ], local_sem=S.snt)
-    sent += 2 * (len(ex) + len(ey))
     g.wait_ge(S.mm0, 1)
     g.wait_ge(S.mm1, 1)
     tx, ty = info[twin]["relay"]
@@ -132,18 +127,15 @@ def _rank(g, core, T, topo, info):
         RemoteDMATransfer(dst_ids=[_dst(topo, tx, core)], dma_engine_mask=ex[0], remote_sem=S.cr),
         RemoteDMATransfer(dst_ids=[_dst(topo, ty, core)], dma_engine_mask=ey[0], remote_sem=S.cr),
     ], local_sem=S.snt)
-    sent += 2
+    g.wait_ge(S.ldc, 32)
     g.remote_dma_fused([
-        RemoteDMATransfer(dst_ids=[dp], dma_engine_mask=_join(e0), remote_sem=S.n0, src=T.op0[:], dst=T.wp[:, 2 * TW:3 * TW]),
-        RemoteDMATransfer(dst_ids=[dp], dma_engine_mask=_join(e1), remote_sem=S.n1, src=T.op1[:], dst=T.np1[:]),
-    ], local_sem=S.snt)
-    g.remote_dma_fused([
+        RemoteDMATransfer(dst_ids=[dx], dma_engine_mask=_join(ex), remote_sem=S.rlc, src=_c8(T.oc0[:]), dst=_c8(T.rc[:])),
+        RemoteDMATransfer(dst_ids=[dy], dma_engine_mask=_join(ey), remote_sem=S.rlc, src=_c8(T.oc1[:]), dst=_c8(T.rc[:])),
         RemoteDMATransfer(dst_ids=[dp], dma_engine_mask=_join(e0), remote_sem=S.n0, src=_c8(T.oc0[:]),
                           dst=_c8(T.wq[:, 2 * TW:3 * TW])),
         RemoteDMATransfer(dst_ids=[dp], dma_engine_mask=_join(e1), remote_sem=S.n1, src=_c8(T.oc1[:]), dst=_c8(T.nc1[:])),
     ], local_sem=S.snt)
-    sent += 2 * (len(e0) + len(e1))
-    g.wait_ge(S.snt, sent)
+    g.wait_ge(S.snt, 2 * (len(ex) + len(ey) + len(e0) + len(e1)) + 2)
 
     nrel = 2 * len(_bits(topo.mask(info[twin]["relay"][0], core)))
     st_, so_ = "r%d" % info[twin]["pos"], "r%d" % info[other]["pos"]

@@ -17,10 +17,11 @@ SCRATCH = {
     "rc": ("dram", [128, TW], "float8_e4m3fn_x4"), "rp": ("dram", [128, TW], "uint8"),
     "fc0": ("dram", [128, TW], "float8_e4m3fn_x4"), "fc1": ("dram", [128, TW], "float8_e4m3fn_x4"),
     "fp0": ("dram", [128, TW], "uint8"), "fp1": ("dram", [128, TW], "uint8"),
-    "nc1": ("dram", [128, TW], "float8_e4m3fn_x4"), "np1": ("dram", [128, TW], "uint8"),
+    "nc0": ("dram", [128, TW], "float8_e4m3fn_x4"), "nc1": ("dram", [128, TW], "float8_e4m3fn_x4"),
+    "np0": ("dram", [128, TW], "uint8"), "np1": ("dram", [128, TW], "uint8"),
 }
-SEMAPHORES = (["ldp", "ldc", "ldx", "ldw", "qz", "snt", "rlp", "rlc", "cr", "n0", "n1", "r00", "r01", "r10", "r11",
-               "f3", "f6", "f7"]
+SEMAPHORES = (["ldp", "ldc", "ldx", "qz", "snt", "rlp", "rlc", "a0p", "a1p", "a0c", "a1c",
+               "p00", "p01", "p10", "p11", "r00", "r01", "r10", "r11", "f0", "f1", "f2", "f3", "f6", "f7"]
               + ["mm%d" % k for k in range(8)] + ["cp%d" % k for k in range(8)] + ["st%d" % k for k in range(8)])
 
 
@@ -80,14 +81,13 @@ def _relay(g, core, T, topo, info, s, i):
     twin, other = info[s]["twin"], info[s]["other"]
     bits = _bits(topo.mask(core, twin) & topo.mask(core, other))
     mask = _join(bits)
-    sem = S["r%d%d" % (info[s]["pos"], i)]
+    tag = "%d%d" % (info[s]["pos"], i)
     ids = [_dst(topo, twin, core), _dst(topo, other, core)]
-    g.wait_ge(S.rlp, 4)
-    g.wait_ge(S.cr, 1)
-    g.remote_dma_fused([RemoteDMATransfer(dst_ids=ids, dma_engine_mask=mask, remote_sem=sem, srcs=[T.rp[:]],
+    g.wait_ge(S.rlp, 1)
+    g.remote_dma_fused([RemoteDMATransfer(dst_ids=ids, dma_engine_mask=mask, remote_sem=S["p" + tag], srcs=[T.rp[:]],
                                           dsts=[T.wp[:, TW * i:TW * i + TW], T["fp%d" % i][:]])], local_sem=S.snt)
     g.wait_ge(S.rlc, 4)
-    g.remote_dma_fused([RemoteDMATransfer(dst_ids=ids, dma_engine_mask=mask, remote_sem=sem, srcs=[_c8(T.rc[:])],
+    g.remote_dma_fused([RemoteDMATransfer(dst_ids=ids, dma_engine_mask=mask, remote_sem=S["r" + tag], srcs=[_c8(T.rc[:])],
                                           dsts=[_c8(T.wq[:, TW * i:TW * i + TW]), _c8(T["fc%d" % i][:])])], local_sem=S.snt)
     g.wait_ge(S.snt, 2 * len(bits))
 
@@ -100,13 +100,13 @@ def _rank(g, core, T, topo, info):
     peer, twin, other = me["peer"], me["twin"], me["other"]
     rx, ry = me["relay"]
 
-    g.scalar.dma_start(T.op0[:], T.ws[:, 0:TW]).then_inc(S.ldp, 16)
+    g.sync.dma_start(T.op0[:], T.ws[:, 0:TW]).then_inc(S.ldp, 16)
     g.scalar.dma_start(T.op1[:], T.ws[:, TW:2 * TW]).then_inc(S.ldp, 16)
     g.sync.dma_start(_c8(T.oc0[:]), T.wc[:, 0:4 * TW]).then_inc(S.ldc, 16)
-    g.sync.dma_start(_c8(T.oc1[:]), T.wc[:, 4 * TW:8 * TW]).then_inc(S.ldc, 16)
+    g.scalar.dma_start(_c8(T.oc1[:]), T.wc[:, 4 * TW:8 * TW]).then_inc(S.ldc, 16)
     g.scalar.dma_start(T.xb[:], T.x[:]).then_inc(S.ldx, 16)
-    g.sync.dma_start(_c8(T.wq[:, 0:2 * TW]), T.wc[:]).then_inc(S.ldw, 16)
-    g.scalar.dma_start(T.wp[:, 0:2 * TW], T.ws[:]).then_inc(S.ldw, 16)
+    g.sync.dma_start(_c8(T.wq[:, 2 * TW:3 * TW]), T.wc[:, 0:4 * TW]).then_inc(S.f0, 16)
+    g.scalar.dma_start(T.wp[:, 2 * TW:3 * TW], T.ws[:, 0:TW]).then_inc(S.f0, 16)
 
     off = _bits(topo.mask(core, rx) & topo.mask(core, ry))
     ex, ey = off[0::2], off[1::2]
@@ -115,38 +115,30 @@ def _rank(g, core, T, topo, info):
     dx, dy, dp = _dst(topo, rx, core), _dst(topo, ry, core), _dst(topo, peer, core)
     g.wait_ge(S.ldp, 32)
     g.remote_dma_fused([
-        RemoteDMATransfer(dst_ids=[dx], dma_engine_mask=_join(ex), remote_sem=S.rlp, src=T.op0[:], dst=T.rp[:]),
-        RemoteDMATransfer(dst_ids=[dy], dma_engine_mask=_join(ey), remote_sem=S.rlp, src=T.op1[:], dst=T.rp[:]),
-        RemoteDMATransfer(dst_ids=[dp], dma_engine_mask=_join(e0), remote_sem=S.n0, src=T.op0[:], dst=T.wp[:, 2 * TW:3 * TW]),
-        RemoteDMATransfer(dst_ids=[dp], dma_engine_mask=_join(e1), remote_sem=S.n1, src=T.op1[:], dst=T.np1[:]),
-    ], local_sem=S.snt)
-    g.wait_ge(S.mm0, 1)
-    g.wait_ge(S.mm1, 1)
-    tx, ty = info[twin]["relay"]
-    g.remote_dma_fused([
-        RemoteDMATransfer(dst_ids=[_dst(topo, tx, core)], dma_engine_mask=ex[0], remote_sem=S.cr),
-        RemoteDMATransfer(dst_ids=[_dst(topo, ty, core)], dma_engine_mask=ey[0], remote_sem=S.cr),
+        RemoteDMATransfer(dst_ids=[dx], dma_engine_mask=ex[0], remote_sem=S.rlp, src=T.op0[:], dst=T.rp[:]),
+        RemoteDMATransfer(dst_ids=[dy], dma_engine_mask=ey[0], remote_sem=S.rlp, src=T.op1[:], dst=T.rp[:]),
+        RemoteDMATransfer(dst_ids=[dp], dma_engine_mask=e0[0], remote_sem=S.a0p, src=T.op0[:], dst=T.np0[:]),
+        RemoteDMATransfer(dst_ids=[dp], dma_engine_mask=e1[0], remote_sem=S.a1p, src=T.op1[:], dst=T.np1[:]),
     ], local_sem=S.snt)
     g.wait_ge(S.ldc, 32)
     g.remote_dma_fused([
         RemoteDMATransfer(dst_ids=[dx], dma_engine_mask=_join(ex), remote_sem=S.rlc, src=_c8(T.oc0[:]), dst=_c8(T.rc[:])),
         RemoteDMATransfer(dst_ids=[dy], dma_engine_mask=_join(ey), remote_sem=S.rlc, src=_c8(T.oc1[:]), dst=_c8(T.rc[:])),
-        RemoteDMATransfer(dst_ids=[dp], dma_engine_mask=_join(e0), remote_sem=S.n0, src=_c8(T.oc0[:]),
-                          dst=_c8(T.wq[:, 2 * TW:3 * TW])),
-        RemoteDMATransfer(dst_ids=[dp], dma_engine_mask=_join(e1), remote_sem=S.n1, src=_c8(T.oc1[:]), dst=_c8(T.nc1[:])),
+        RemoteDMATransfer(dst_ids=[dp], dma_engine_mask=_join(e0), remote_sem=S.a0c, src=_c8(T.oc0[:]), dst=_c8(T.nc0[:])),
+        RemoteDMATransfer(dst_ids=[dp], dma_engine_mask=_join(e1), remote_sem=S.a1c, src=_c8(T.oc1[:]), dst=_c8(T.nc1[:])),
     ], local_sem=S.snt)
-    g.wait_ge(S.snt, 2 * (len(ex) + len(ey) + len(e0) + len(e1)) + 2)
+    g.wait_ge(S.snt, 4 + len(ex) + len(ey) + len(e0) + len(e1))
 
-    nrel = 2 * len(_bits(topo.mask(info[twin]["relay"][0], core)))
-    st_, so_ = "r%d" % info[twin]["pos"], "r%d" % info[other]["pos"]
+    nrel = len(_bits(topo.mask(info[twin]["relay"][0], core)))
+    tt, to = "%d" % info[twin]["pos"], "%d" % info[other]["pos"]
     rp_, rt_, ro_ = cores.index(peer), cores.index(twin), cores.index(other)
     blocks = [
-        (0, r, 0, [(S.qz, 1), (S.ldw, 32)]),
-        (1, r, 1, []),
-        (2, rp_, 0, [(S.n0, 2 * len(e0))]),
+        (2, r, 0, [(S.qz, 1), (S.f0, 32)]),
+        (2, r, 1, [(S.f1, 32)]),
+        (2, rp_, 0, [(S.f2, 32)]),
         (2, rp_, 1, [(S.f3, 32)]),
-        (0, rt_, 0, [(S[st_ + "0"], nrel)]),
-        (1, rt_, 1, [(S[st_ + "1"], nrel)]),
+        (0, rt_, 0, [(S["p" + tt + "0"], nrel), (S["r" + tt + "0"], nrel)]),
+        (1, rt_, 1, [(S["p" + tt + "1"], nrel), (S["r" + tt + "1"], nrel)]),
         (2, ro_, 0, [(S.f6, 32)]),
         (0, ro_, 1, [(S.f7, 32)]),
     ]
@@ -172,21 +164,36 @@ def _rank(g, core, T, topo, info):
 
     def fetch(q, codes, src, slot, free, arrived, count, done):
         q.wait_ge(free, 1)
-        q.wait_ge(arrived, count)
+        if arrived is not None:
+            q.wait_ge(arrived, count)
         if codes:
-            q.dma_start(_c8(T.wq[:, TW * slot:TW * slot + TW]), _c8(src[:])).then_inc(done, 16)
+            q.dma_start(_c8(T.wq[:, TW * slot:TW * slot + TW]), src).then_inc(done, 16)
         else:
-            q.dma_start(T.wp[:, TW * slot:TW * slot + TW], src[:]).then_inc(done, 16)
+            q.dma_start(T.wp[:, TW * slot:TW * slot + TW], src).then_inc(done, 16)
 
-    for q, codes, odd in ((g.sync, True, 0), (g.scalar, False, 1)):
-        store(q, 0 + odd)
-        fetch(q, codes, T.nc1 if codes else T.np1, 2, S.mm2, S.n1, 2 * len(e1), S.f3)
-        store(q, 2 + odd)
-        fetch(q, codes, T.fc0 if codes else T.fp0, 2, S.mm3, S[so_ + "0"], nrel, S.f6)
-        fetch(q, codes, T.fc1 if codes else T.fp1, 0, S.mm4, S[so_ + "1"], nrel, S.f7)
-        store(q, 4 + odd)
-        store(q, 6 + odd)
-        q.wait_ge(S["st%d" % (6 + odd)], 16)
+    q = g.sync
+    fetch(q, True, T.wc[:, 4 * TW:8 * TW], 2, S.mm0, None, 0, S.f1)
+    store(q, 0)
+    fetch(q, True, _c8(T.nc0[:]), 2, S.mm1, S.a0c, len(e0), S.f2)
+    fetch(q, True, _c8(T.nc1[:]), 2, S.mm2, S.a1c, len(e1), S.f3)
+    store(q, 2)
+    fetch(q, True, _c8(T.fc0[:]), 2, S.mm3, S["r" + to + "0"], nrel, S.f6)
+    fetch(q, True, _c8(T.fc1[:]), 0, S.mm4, S["r" + to + "1"], nrel, S.f7)
+    store(q, 4)
+    store(q, 6)
+    q.wait_ge(S.st6, 16)
+
+    q = g.scalar
+    fetch(q, False, T.ws[:, TW:2 * TW], 2, S.mm0, None, 0, S.f1)
+    store(q, 1)
+    fetch(q, False, T.np0[:], 2, S.mm1, S.a0p, 1, S.f2)
+    fetch(q, False, T.np1[:], 2, S.mm2, S.a1p, 1, S.f3)
+    store(q, 3)
+    fetch(q, False, T.fp0[:], 2, S.mm3, S["p" + to + "0"], nrel, S.f6)
+    fetch(q, False, T.fp1[:], 0, S.mm4, S["p" + to + "1"], nrel, S.f7)
+    store(q, 5)
+    store(q, 7)
+    q.wait_ge(S.st7, 16)
 
 
 def rank_program(g, core, T, topo):

from concourse.bass import DstId, RemoteDMATransfer
from concourse.mybir import dt

NHOSTS = 4
TW = 128

SCRATCH = {
    "xb": ("sbuf", [128, 512], "bfloat16"),
    "xq": ("sbuf", [128, TW], "float8_e4m3fn_x4"),
    "xs": ("sbuf", [128, TW], "uint8"),
    "wq": ("sbuf", [128, 3 * TW], "float8_e4m3fn_x4"),
    "wp": ("sbuf", [128, 3 * TW], "uint8"),
    "st": ("sbuf", [128, 2 * TW], "float32"),
    "ps": ("psum", [128, 8 * 512], "float32"),
    "oc0": ("dram", [128, TW], "float8_e4m3fn_x4"), "oc1": ("dram", [128, TW], "float8_e4m3fn_x4"),
    "op0": ("dram", [128, TW], "uint8"), "op1": ("dram", [128, TW], "uint8"),
    "rc": ("dram", [128, TW], "float8_e4m3fn_x4"), "rp": ("dram", [128, TW], "uint8"),
    "fc0": ("dram", [128, TW], "float8_e4m3fn_x4"), "fc1": ("dram", [128, TW], "float8_e4m3fn_x4"),
    "fp0": ("dram", [128, TW], "uint8"), "fp1": ("dram", [128, TW], "uint8"),
    "nc0": ("dram", [128, TW], "float8_e4m3fn_x4"), "nc1": ("dram", [128, TW], "float8_e4m3fn_x4"),
    "np0": ("dram", [128, TW], "uint8"), "np1": ("dram", [128, TW], "uint8"),
}
SEMAPHORES = (["ldp", "ldc", "ldx", "qz", "snt", "rlp", "rlc", "a0p", "a1p", "a0c", "a1c",
               "p00", "p01", "p10", "p11", "r00", "r01", "r10", "r11", "f0", "f1", "f2", "f3", "f6", "f7"]
              + ["mm%d" % k for k in range(8)] + ["cp%d" % k for k in range(8)] + ["st%d" % k for k in range(8)])


def _bits(mask):
    return [1 << k for k in range(mask.bit_length()) if (mask >> k) & 1]


def _join(bits):
    m = 0
    for b in bits:
        m |= b
    return m


def _c8(ap):
    return ap.bitcast(dt.uint8)


def _plan(T, topo):
    cores = list(T.cores)
    per = topo.CORES_PER_HOST
    info, relay = {}, {}
    for s in cores:
        here = [c for c in cores if topo.host(c) == topo.host(s)]
        far = [c for c in cores if topo.host(c) != topo.host(s)]
        twin = [c for c in far if topo.die(c) == topo.die(s)][0]
        other = [c for c in far if c != twin][0]
        mids = []
        for m in range(NHOSTS):
            image = s % per + m * per
            if m in (topo.host(s), topo.host(twin)):
                continue
            if topo.may_write(s, image) and topo.may_write(image, twin):
                mids.append(m)
        rel = []
        for m in mids[:2]:
            images = [c % per + m * per for c in cores]
            if topo.rack(m) == topo.rack(topo.host(s)):
                k = s % per + m * per
            else:
                k = [c for c in range(m * per, (m + 1) * per)
                     if topo.chip(c) == topo.chip(s) and topo.die(c) == topo.die(s) and c not in images][0]
            rel.append(k)
        info[s] = {"peer": [c for c in here if c != s][0], "twin": twin, "other": other, "pos": here.index(s), "relay": rel}
        for i, k in enumerate(rel):
            relay[k] = (s, i)
    return info, relay


def _dst(topo, d, src):
    rid, pid = topo.addr(d, src)
    return DstId(rid=rid, pnc=pid)


def _relay(g, core, T, topo, info, s, i):
    S = T.sem
    twin, other = info[s]["twin"], info[s]["other"]
    bits = _bits(topo.mask(core, twin) & topo.mask(core, other))
    mask = _join(bits)
    tag = "%d%d" % (info[s]["pos"], i)
    ids = [_dst(topo, twin, core), _dst(topo, other, core)]
    g.wait_ge(S.rlp, 1)
    g.remote_dma_fused([RemoteDMATransfer(dst_ids=ids, dma_engine_mask=mask, remote_sem=S["p" + tag], srcs=[T.rp[:]],
                                          dsts=[T.wp[:, TW * i:TW * i + TW], T["fp%d" % i][:]])], local_sem=S.snt)
    g.wait_ge(S.rlc, 4)
    g.remote_dma_fused([RemoteDMATransfer(dst_ids=ids, dma_engine_mask=mask, remote_sem=S["r" + tag], srcs=[_c8(T.rc[:])],
                                          dsts=[_c8(T.wq[:, TW * i:TW * i + TW]), _c8(T["fc%d" % i][:])])], local_sem=S.snt)
    g.wait_ge(S.snt, 2 * len(bits))


def _rank(g, core, T, topo, info):
    S = T.sem
    me = info[core]
    cores = list(T.cores)
    r = T.rank_of(core)
    peer, twin, other = me["peer"], me["twin"], me["other"]
    rx, ry = me["relay"]

    g.sync.dma_start(T.op0[:], T.ws[:, 0:TW]).then_inc(S.ldp, 16)
    g.scalar.dma_start(T.op1[:], T.ws[:, TW:2 * TW]).then_inc(S.ldp, 16)
    g.sync.dma_start(_c8(T.oc0[:]), T.wc[:, 0:4 * TW]).then_inc(S.ldc, 16)
    g.scalar.dma_start(_c8(T.oc1[:]), T.wc[:, 4 * TW:8 * TW]).then_inc(S.ldc, 16)
    g.scalar.dma_start(T.xb[:], T.x[:]).then_inc(S.ldx, 16)
    g.sync.dma_start(_c8(T.wq[:, 2 * TW:3 * TW]), T.wc[:, 0:4 * TW]).then_inc(S.f0, 16)
    g.scalar.dma_start(T.wp[:, 2 * TW:3 * TW], T.ws[:, 0:TW]).then_inc(S.f0, 16)

    off = _bits(topo.mask(core, rx) & topo.mask(core, ry))
    ex, ey = off[0::2], off[1::2]
    near = [b for b in _bits(topo.mask(core, peer)) if b not in off]
    e0, e1 = near[0::2], near[1::2]
    dx, dy, dp = _dst(topo, rx, core), _dst(topo, ry, core), _dst(topo, peer, core)
    g.wait_ge(S.ldp, 32)
    g.remote_dma_fused([
        RemoteDMATransfer(dst_ids=[dx], dma_engine_mask=ex[0], remote_sem=S.rlp, src=T.op0[:], dst=T.rp[:]),
        RemoteDMATransfer(dst_ids=[dy], dma_engine_mask=ey[0], remote_sem=S.rlp, src=T.op1[:], dst=T.rp[:]),
        RemoteDMATransfer(dst_ids=[dp], dma_engine_mask=e0[0], remote_sem=S.a0p, src=T.op0[:], dst=T.np0[:]),
        RemoteDMATransfer(dst_ids=[dp], dma_engine_mask=e1[0], remote_sem=S.a1p, src=T.op1[:], dst=T.np1[:]),
    ], local_sem=S.snt)
    g.wait_ge(S.ldc, 32)
    g.remote_dma_fused([
        RemoteDMATransfer(dst_ids=[dx], dma_engine_mask=_join(ex), remote_sem=S.rlc, src=_c8(T.oc0[:]), dst=_c8(T.rc[:])),
        RemoteDMATransfer(dst_ids=[dy], dma_engine_mask=_join(ey), remote_sem=S.rlc, src=_c8(T.oc1[:]), dst=_c8(T.rc[:])),
        RemoteDMATransfer(dst_ids=[dp], dma_engine_mask=_join(e0), remote_sem=S.a0c, src=_c8(T.oc0[:]), dst=_c8(T.nc0[:])),
        RemoteDMATransfer(dst_ids=[dp], dma_engine_mask=_join(e1), remote_sem=S.a1c, src=_c8(T.oc1[:]), dst=_c8(T.nc1[:])),
    ], local_sem=S.snt)
    g.wait_ge(S.snt, 4 + len(ex) + len(ey) + len(e0) + len(e1))

    nrel = len(_bits(topo.mask(info[twin]["relay"][0], core)))
    tt, to = "%d" % info[twin]["pos"], "%d" % info[other]["pos"]
    rp_, rt_, ro_ = cores.index(peer), cores.index(twin), cores.index(other)
    blocks = [
        (2, r, 0, [(S.qz, 1), (S.f0, 32)]),
        (2, r, 1, [(S.f1, 32)]),
        (2, rp_, 0, [(S.f2, 32)]),
        (2, rp_, 1, [(S.f3, 32)]),
        (0, rt_, 0, [(S["p" + tt + "0"], nrel), (S["r" + tt + "0"], nrel)]),
        (1, rt_, 1, [(S["p" + tt + "1"], nrel), (S["r" + tt + "1"], nrel)]),
        (2, ro_, 0, [(S.f6, 32)]),
        (0, ro_, 1, [(S.f7, 32)]),
    ]
    g.vector.wait_ge(S.ldx, 16)
    g.vector.quantize_mx(T.xq[:], T.xs[:], T.xb[:]).then_inc(S.qz, 1)
    for k, (slot, j, i, waits) in enumerate(blocks):
        b = 2 * j + i
        for sem, val in waits:
            g.tensor.wait_ge(sem, val)
        g.tensor.matmul_mx(T.ps[:, 512 * b:512 * b + TW], T.wq[:, TW * slot:TW * slot + TW], T.wp[:, TW * slot:TW * slot + TW],
                           T.xq[:], T.xs[:], True, True).then_inc(S["mm%d" % k], 1)
        g.vector.wait_ge(S["mm%d" % k], 1)
        if k >= 2:
            g.vector.wait_ge(S["st%d" % (k - 2)], 16)
        h = k % 2
        g.vector.tensor_copy(T.st[:, TW * h:TW * h + TW], T.ps[:, 512 * b:512 * b + TW]).then_inc(S["cp%d" % k], 1)

    def store(q, k):
        b = 2 * blocks[k][1] + blocks[k][2]
        h = k % 2
        q.wait_ge(S["cp%d" % k], 1)
        q.dma_start(T.y[:, TW * b:TW * b + TW], T.st[:, TW * h:TW * h + TW]).then_inc(S["st%d" % k], 16)

    def fetch(q, codes, src, slot, free, arrived, count, done):
        q.wait_ge(free, 1)
        if arrived is not None:
            q.wait_ge(arrived, count)
        if codes:
            q.dma_start(_c8(T.wq[:, TW * slot:TW * slot + TW]), src).then_inc(done, 16)
        else:
            q.dma_start(T.wp[:, TW * slot:TW * slot + TW], src).then_inc(done, 16)

    q = g.sync
    fetch(q, True, T.wc[:, 4 * TW:8 * TW], 2, S.mm0, None, 0, S.f1)
    store(q, 0)
    fetch(q, True, _c8(T.nc0[:]), 2, S.mm1, S.a0c, len(e0), S.f2)
    fetch(q, True, _c8(T.nc1[:]), 2, S.mm2, S.a1c, len(e1), S.f3)
    store(q, 2)
    fetch(q, True, _c8(T.fc0[:]), 2, S.mm3, S["r" + to + "0"], nrel, S.f6)
    fetch(q, True, _c8(T.fc1[:]), 0, S.mm4, S["r" + to + "1"], nrel, S.f7)
    store(q, 4)
    store(q, 6)
    q.wait_ge(S.st6, 16)

    q = g.scalar
    fetch(q, False, T.ws[:, TW:2 * TW], 2, S.mm0, None, 0, S.f1)
    store(q, 1)
    fetch(q, False, T.np0[:], 2, S.mm1, S.a0p, 1, S.f2)
    fetch(q, False, T.np1[:], 2, S.mm2, S.a1p, 1, S.f3)
    store(q, 3)
    fetch(q, False, T.fp0[:], 2, S.mm3, S["p" + to + "0"], nrel, S.f6)
    fetch(q, False, T.fp1[:], 0, S.mm4, S["p" + to + "1"], nrel, S.f7)
    store(q, 5)
    store(q, 7)
    q.wait_ge(S.st7, 16)


def rank_program(g, core, T, topo):
    info, relay = _plan(T, topo)
    if core in relay:
        s, i = relay[core]
        _relay(g, core, T, topo, info, s, i)
    elif T.rank_of(core) is not None:
        _rank(g, core, T, topo, info)
